import numpy as np
import ml_dtypes


def mxq(x, axis, fmt="e4m3"):
    dtype, down = {"e4m3": (ml_dtypes.float8_e4m3fn, 7), "e5m2": (ml_dtypes.float8_e5m2, 14)}[fmt]
    v = np.moveaxis(np.asarray(x, np.float32).astype(ml_dtypes.bfloat16).astype(np.float64), axis, -1)
    blocks = v.reshape(v.shape[:-1] + (-1, 32))
    amax = np.abs(blocks).max(-1, keepdims=True)
    byte = np.maximum(np.where(amax > 0, np.frexp(amax)[1] - 1 + 127, 0) - down, 1)
    scale = np.exp2(byte - 127.0)
    codes = (blocks / scale).astype(np.float32).astype(dtype).astype(np.float64)
    return np.moveaxis((codes * scale).reshape(v.shape), -1, axis)


WIDE = False


def mx_kscale(k):
    if not WIDE:
        return np.ones(k)
    levels = np.array([10, -10, 5, -5, 0])
    if k % 512:
        return np.exp2(np.random.permutation(np.resize(levels, k // 32))).repeat(32)
    a = np.empty((k // 512, 16))
    for p in range(k // 512):
        a[p, :8] = np.random.permutation(np.resize(levels, 8))
        for g in range(8):
            far = levels[np.abs(levels - a[p, g]) >= 10]
            a[p, g + 8] = far[np.random.randint(len(far))]
    return np.exp2(a.ravel()).repeat(32)


def f64(x):
    return np.asarray(x).astype(np.float64)


def striped(idx):
    return np.tile(idx.reshape(-1, 16).T, (8, 1)).astype(np.uint16)


def unstriped(offs):
    return offs[:16].T.reshape(-1).astype(np.int64)


E2M1 = np.array([0.0, 0.5, 1.0, 1.5, 2.0, 3.0, 4.0, 6.0, -0.0, -0.5, -1.0, -1.5, -2.0, -3.0, -4.0, -6.0])


def pack_weight(w, fmt):
    k, n = w.shape
    w = f64(np.asarray(w, np.float32).astype(ml_dtypes.bfloat16)).reshape(k // 32, 32, n)
    amax = np.abs(w).max(1)
    if fmt == "e4m3":
        byte = np.frexp(amax)[1] - 1 + 127 - 7
    else:
        mant, ex = np.frexp(amax / 6.0)
        byte = np.where(mant > 0.5, ex, ex - 1) + 127
    byte = np.clip(np.where(amax > 0, byte, 1), 1, 254)
    scaled = (w * np.exp2(127.0 - byte)[:, None, :]).reshape(k, n).astype(np.float32)
    by_word = np.ascontiguousarray(scaled.reshape(k // 512, 128, 4, n).transpose(0, 1, 3, 2))
    if fmt == "e4m3":
        words = by_word.astype(ml_dtypes.float8_e4m3fn).view(np.uint8)
    else:
        c = by_word.astype(ml_dtypes.float4_e2m1fn).view(np.uint8) & 0xF
        words = (c[..., 0::2] | (c[..., 1::2] << 4)).reshape(k // 512, 128, 2 * n)
    return np.ascontiguousarray(words), np.ascontiguousarray(byte.astype(np.uint8).reshape(k // 512, 16, n))


def unpack_weight(words, scales, fmt):
    g, _, n = scales.shape
    words = np.ascontiguousarray(words).reshape(g, 128, n, -1)
    if fmt == "e4m3":
        vals = words.view(ml_dtypes.float8_e4m3fn).astype(np.float64)
    else:
        nib = np.empty((g, 128, n, 4), np.uint8)
        nib[..., 0::2] = words & 0xF
        nib[..., 1::2] = words >> 4
        vals = E2M1[nib]
    vals = vals * np.repeat(np.exp2(scales.astype(np.float64) - 127.0), 8, axis=1)[..., None]
    return vals.transpose(0, 1, 3, 2).reshape(g * 512, n)


def gelu(v):
    return 0.5 * v * (1.0 + np.tanh(np.sqrt(2.0 / np.pi) * (v + 0.044715 * v**3)))


def striped8(idx):
    return np.concatenate([v.reshape(-1, 16).T for v in idx]).astype(np.uint16)


def unstriped8(offs):
    return np.stack([offs[16 * g:16 * g + 16].T.reshape(-1) for g in range(8)]).astype(np.int64)


def runs(v, idx8):
    k = np.arange(v.shape[0])
    return v[k[:, None], idx8[k % 512 // 64]]


def bf(x):
    return np.asarray(x, np.float32).astype(ml_dtypes.bfloat16)


def planes(Y):
    n, m = Y.shape
    b = f64(bf(Y)).reshape(n // 32, 32, m)
    amax = np.abs(b).max(1)
    byte = np.clip(np.where(amax > 0, np.frexp(amax)[1] - 1 + 127 - 7, 1), 1, 254)
    codes = (b * np.exp2(127.0 - byte)[:, None, :]).reshape(n, m).astype(np.float32).astype(ml_dtypes.float8_e4m3fn).view(np.uint8)
    words = codes.reshape(n // 512, 128, 4, m).transpose(0, 1, 3, 2)
    return np.ascontiguousarray(words), np.ascontiguousarray(byte.astype(np.uint8).reshape(n // 512, 16, m))


K, T, S, P, H, N = 1536, 2048, 1024, 512, 512, 1024

def setup_inputs():
    n = np.random.standard_normal
    s = mx_kscale(K)[:, None]
    u = mx_kscale(H)[:, None]
    d = {}
    d["tab_words"], d["tab_scales"] = pack_weight(n((K, T)) * s, "e4m3")
    d["offs"] = striped8(np.stack([np.random.permutation(T)[:S] for _ in range(8)]))
    d["w1_words"], d["w1_scales"] = pack_weight(5.0 * n((K, H)) / K ** 0.5 / s * (u * u).T, "e2m1")
    d["level"] = (np.exp(0.5 * n(H)) * u[:, 0] * u[:, 0]).astype(np.float32)
    d["w2"] = (1.2 * n((K, H)) / K ** 0.5 / s * u.T).astype(np.float32)
    d["pos1"] = striped(np.random.permutation(S)[:P])
    d["pos2"] = striped(np.random.permutation(S)[:P])
    d["allow"] = (1.2 * n((H, P)) * u).astype(np.float32)
    d["w3"] = (0.6 * n((H, N)) / H ** 0.5 / u).astype(np.float32)
    d["rowgain"] = np.exp(0.8 * n(N)).astype(np.float32)
    return d

def reference(tab_words, tab_scales, offs, w1_words, w1_scales, level, w2, pos1, pos2, allow, w3, rowgain):
    v = runs(unpack_weight(tab_words, tab_scales, "e4m3"), unstriped8(offs))
    w1 = unpack_weight(w1_words, w1_scales, "e2m1")
    a = w1.T @ v
    b = mxq(f64(w2), 0, "e4m3").T @ v
    h = np.sqrt(f64(level)[:, None] + np.abs(a)) + b
    z = np.minimum(h[:, unstriped(pos1)] + f64(allow), h[:, unstriped(pos2)])
    y = f64(rowgain)[:, None] * (mxq(f64(w3), 0, "e4m3").T @ mxq(z, 0, "e4m3"))
    words, scales = planes(y)
    return y, words, scales

@@ -1,0 +1,281 @@
+from contextlib import ExitStack
+
+import concourse.mybir as mybir
+
+K, T, S, PAIRS, H, N = 1536, 2048, 1024, 512, 512, 1024
+FLOPS = 2 * (2 * K * H * S + H * N * PAIRS)
+
+F32 = mybir.dt.float32
+BF16 = mybir.dt.bfloat16
+I32 = mybir.dt.int32
+U32 = mybir.dt.uint32
+U16 = mybir.dt.uint16
+U8 = mybir.dt.uint8
+E4M3 = mybir.dt.float8_e4m3fn_x4
+E2M1 = mybir.dt.float4_e2m1fn_x4
+ACT = mybir.ActivationFunctionType
+ALU = mybir.AluOpType
+
+P = 128
+PASSES = K // 512
+BANK = 512
+HALF = PAIRS // 2
+
+
+def tile_list_still_cut_features_kernel(
+    tc, tab_words, tab_scales, offs, w1_words, w1_scales, level, w2, pos1, pos2, allow, w3, rowgain,
+    out_0, out_1, out_2,
+):
+    nc = tc.nc
+    with ExitStack() as ctx:
+        keep = ctx.enter_context(tc.tile_pool(name="keep", bufs=1))
+        ring = ctx.enter_context(tc.tile_pool(name="ring", bufs=2))
+        psum = ctx.enter_context(tc.psum_pool(name="psum", bufs=4))
+
+        def held(shape, dtype, name):
+            return keep.tile(shape, dtype, name=name, align_bytes=64)
+
+        offs_t = keep.tile([P, S // 16], U16, name="offs_t")
+        pos1_t = keep.tile([P, PAIRS // 16], U16, name="pos1_t")
+        pos2_t = keep.tile([P, PAIRS // 16], U16, name="pos2_t")
+        nc.sync.dma_start(offs_t[:], offs)
+        nc.sync.dma_start(pos1_t[:], pos1)
+        nc.sync.dma_start(pos2_t[:], pos2)
+
+        def staged(shape, dtype, name, tag):
+            return keep.tile(shape, dtype, name=name, tag=tag, align_bytes=64)
+
+        sc_win = staged([P, T], U8, "sc_win", "z")
+        nc.gpsimd.memset(sc_win[:].bitcast(I32), 0)
+        v_planes = held([P, PASSES * S], U8, "v_planes")
+        nc.vector.memset(v_planes[:].bitcast(I32), 0)
+        w1_sc_raw = staged([P, PASSES * H], U8, "w1_sc_raw", "small")
+        nc.gpsimd.memset(w1_sc_raw[:].bitcast(I32), 0)
+        nc.scalar.dma_start(
+            sc_win[0:P:4, :].bitcast(I32), tab_scales[0:2].bitcast(I32).rearrange("a q t -> q a t")
+        )
+        nc.scalar.dma_start(sc_win[2:P:8, :].bitcast(I32), tab_scales[2].bitcast(I32))
+        for d in range(4):
+            nc.gpsimd.dma_start(
+                w1_sc_raw[32 * d:32 * d + 4, :].bitcast(I32).rearrange("r (a c) -> r a c", a=PASSES),
+                w1_scales[:, 4 * d:4 * d + 4, :].bitcast(I32).rearrange("a r c -> r a c"),
+            )
+
+        warm = held([P, 1], F32, "warm")
+        warm2 = held([P, 1], F32, "warm2")
+        nc.gpsimd.memset(warm[:], 1.0)
+        nc.scalar.activation(warm2[:], warm[:], ACT.Sqrt)
+
+        def load_table(a, tag):
+            words = staged([P, T], I32, "tabw%d" % a, tag)
+            nc.sync.dma_start(words[:], tab_words[a].rearrange("p t i -> p (t i)").bitcast(I32))
+            return words
+
+        def load_w2(a, tag):
+            raw = staged([P, 4 * H], F32, "w2_raw%d" % a, tag)
+            nc.sync.dma_start(raw[:], w2[512 * a:512 * (a + 1), :].rearrange("(p j) c -> p (j c)", j=4))
+            return raw
+
+        tab0 = load_table(0, "x")
+        w1_raw = held([P, PASSES * H // 2], I32, "w1_raw")
+        nc.sync.dma_start(
+            w1_raw[:].rearrange("p (a c) -> p a c", a=PASSES),
+            w1_words.bitcast(I32).rearrange("a p c -> p a c"),
+        )
+        tab1 = load_table(1, "y")
+
+        sc_got = held([P, S], U8, "sc_got")
+        nc.vector.tensor_copy(sc_got[:], sc_win[:].indirect(offs_t[:]))
+        for d in range(4):
+            nc.scalar.dma_start(
+                v_planes[32 * d:32 * d + 4, 0:2 * S].bitcast(I32), sc_got[32 * d:32 * d + 32:4, :].bitcast(I32)
+            )
+        for d in range(4):
+            nc.scalar.dma_start(
+                v_planes[32 * d:32 * d + 4, 2 * S:3 * S].bitcast(I32),
+                sc_got[32 * d + 2:32 * d + 32:8, :].bitcast(I32),
+            )
+
+        v_words = [held([P, S], U32, "v_words%d" % a) for a in range(PASSES)]
+        w1_codes = held([P, PASSES * H // 2], I32, "w1_codes")
+        w1_planes = held([P, PASSES * H], U8, "w1_planes")
+        w2_codes = [held([P, H], U32, "w2_codes%d" % a) for a in range(PASSES)]
+        w2_planes = [held([P, H], U8, "w2_planes%d" % a) for a in range(PASSES)]
+
+        def gather_words(a, words):
+            nc.vector.tensor_copy(v_words[a][:], words[:].bitcast(U32).indirect(offs_t[:]))
+
+        def round_w2(copy, raw, lo, hi):
+            w2_bf = ring.tile([P, (hi - lo) * 512], BF16, name="w2_bf", align_bytes=64)
+            copy(
+                w2_bf[:].rearrange("p (t q i j) -> p t q j i", q=16, i=8, j=4),
+                raw[:].rearrange("p (j q t i) -> p t q j i", j=4, t=4, i=8)[:, lo:hi],
+            )
+            return w2_bf
+
+        def quantise_w2(a, lo, hi, w2_bf):
+            nc.vector.quantize_mx(
+                w2_codes[a][:, lo * P:hi * P].bitcast(E4M3), w2_planes[a][:, lo * P:hi * P], w2_bf[:]
+            )
+
+        raw0 = load_w2(0, "z")
+        gather_words(0, tab0)
+        tab2 = load_table(2, "x")
+        nc.vector.tensor_copy(
+            w1_codes[:].rearrange("p (a t q w) -> p a t q w", a=PASSES, t=4, w=4),
+            w1_raw[:].rearrange("p (a q t w) -> p a t q w", a=PASSES, t=4, w=4),
+        )
+        nc.vector.tensor_copy(
+            w1_planes[:].bitcast(I32).rearrange("p (a t q w) -> p a t q w", a=PASSES, t=4, w=2),
+            w1_sc_raw[:].bitcast(I32).rearrange("p (a q t w) -> p a t q w", a=PASSES, t=4, w=2),
+        )
+        small = staged([P, 40], F32, "small", "small")
+        with nc.allow_non_contiguous_dma(reason="one value a partition"):
+            for t in range(4):
+                nc.gpsimd.dma_start(small[:, 8 * t:8 * t + 1], level.rearrange("(q t i) -> t q i", t=4, i=8)[t])
+        gain_t = small[:, 32:40]
+        nc.gpsimd.dma_start(
+            gain_t.rearrange("p (g t) -> p g t", g=2), rowgain.rearrange("(g p t) -> p g t", g=2, t=4)
+        )
+        gather_words(1, tab1)
+        raw1 = load_w2(1, "y")
+        bf0 = round_w2(nc.scalar.copy, raw0, 0, 4)
+        raw2 = load_w2(2, "z")
+        gather_words(2, tab2)
+        allow_t = staged([P, 4 * PAIRS], F32, "allow_t", "x")
+        for t in range(4):
+            nc.sync.dma_start(
+                allow_t[:, t * PAIRS:(t + 1) * PAIRS], allow.rearrange("(q t i) m -> t q (i m)", t=4, i=8)[t]
+            )
+        quantise_w2(0, 0, 4, bf0)
+        quantise_w2(1, 0, 4, round_w2(nc.vector.tensor_copy, raw1, 0, 4))
+        w3_raw = staged([P, 4 * N], F32, "w3_raw", "y")
+        for t in range(4):
+            nc.sync.dma_start(w3_raw[:, t * N:(t + 1) * N], w3.rearrange("(q t i) n -> t q (i n)", t=4, i=8)[t])
+        quantise_w2(2, 0, 2, round_w2(nc.vector.tensor_copy, raw2, 0, 2))
+        quantise_w2(2, 2, 4, round_w2(nc.vector.tensor_copy, raw2, 2, 4))
+
+        def product(tag, t, half, codes, planes):
+            acc = psum.tile([P, BANK], F32, name=tag, tag=tag)
+            for a in range(PASSES):
+                nc.tensor.matmul_mx(
+                    acc[:], lhsT=codes(a, t), lhsT_scale=planes(a, t),
+                    rhs=v_words[a][:, half * BANK:(half + 1) * BANK].bitcast(E4M3),
+                    rhs_scale=v_planes[:, a * S + half * BANK:a * S + (half + 1) * BANK],
+                    start=(a == 0), stop=(a == PASSES - 1),
+                )
+            return acc
+
+        def w1c(a, t):
+            return w1_codes[:].bitcast(U8)[:, 2 * (a * H + t * P):2 * (a * H + (t + 1) * P)].bitcast(E2M1)
+
+        def w1p(a, t):
+            return w1_planes[:, a * H + t * P:a * H + (t + 1) * P]
+
+        def w2c(a, t):
+            return w2_codes[a][:, t * P:(t + 1) * P].bitcast(E4M3)
+
+        def w2p(a, t):
+            return w2_planes[a][:, t * P:(t + 1) * P]
+
+        root = [held([P, S], F32, "root%d" % t) for t in range(4)]
+        for t in range(4):
+            size = ring.tile([P, S], F32, name="size")
+            for half in range(2):
+                acc = product("pa", t, half, w1c, w1p)
+                nc.scalar.activation(size[:, half * BANK:(half + 1) * BANK], acc[:], ACT.Abs)
+            nc.scalar.activation(root[t][:], size[:], ACT.Sqrt, bias=small[:, 8 * t:8 * t + 1])
+
+        cut1 = held([P, 4 * PAIRS], F32, "cut1")
+        cut2 = held([P, 4 * PAIRS], F32, "cut2")
+
+        def pick(h, t, lo, hi):
+            nc.vector.tensor_tensor(
+                cut1[:, t * PAIRS + lo:t * PAIRS + hi], h[:].indirect(pos1_t[:, lo // 16:hi // 16]),
+                allow_t[:, t * PAIRS + lo:t * PAIRS + hi], ALU.add,
+            )
+            nc.vector.tensor_copy(
+                cut2[:, t * PAIRS + lo:t * PAIRS + hi], h[:].indirect(pos2_t[:, lo // 16:hi // 16])
+            )
+
+        h_last = None
+        for t in range(4):
+            h = ring.tile([P, S], F32, name="h")
+            for half in range(2):
+                acc = product("pb", t, half, w2c, w2p)
+                cols = slice(half * BANK, (half + 1) * BANK)
+                nc.vector.tensor_tensor(h[:, cols], acc[:], root[t][:, cols], ALU.add)
+            if t < 3:
+                pick(h, t, 0, PAIRS)
+            h_last = h
+
+        w3_bf = held([P, 4 * N], BF16, "w3_bf")
+        w3_codes = held([P, N], U32, "w3_codes")
+        w3_planes = held([P, N], U8, "w3_planes")
+        for g in range(2):
+            nc.scalar.copy(
+                w3_bf[:, g * 2048:(g + 1) * 2048].rearrange("p (t m j) -> p m j t", t=4, j=4),
+                w3_raw[:].rearrange("p (j g m t) -> p g m j t", j=4, g=2, t=4)[:, g],
+            )
+            nc.vector.quantize_mx(
+                w3_codes[:, g * 512:(g + 1) * 512].bitcast(E4M3), w3_planes[:, g * 512:(g + 1) * 512],
+                w3_bf[:, g * 2048:(g + 1) * 2048],
+            )
+
+        z_codes = []
+        z_planes = []
+        for c in range(2):
+            pick(h_last, 3, c * HALF, (c + 1) * HALF)
+            z_bf = ring.tile([P, 4 * HALF], BF16, name="z_bf", align_bytes=64)
+            view1 = cut1[:].rearrange("p (t c m i) -> p c m t i", t=4, c=2, i=4)[:, c]
+            view2 = cut2[:].rearrange("p (t c m i) -> p c m t i", t=4, c=2, i=4)[:, c]
+            nc.vector.tensor_tensor(z_bf[:].rearrange("p (m i t) -> p m t i", i=4, t=4), view1, view2, ALU.min)
+            zc = held([P, HALF], U32, "z_codes%d" % c)
+            zp = held([P, HALF], U8, "z_planes%d" % c)
+            nc.vector.quantize_mx(zc[:].bitcast(E4M3), zp[:], z_bf[:])
+            z_codes.append(zc)
+            z_planes.append(zp)
+
+        y_planes = held([P, 2 * PAIRS], U8, "y_planes")
+        for c in range(2):
+            y_codes = held([P, 2 * HALF], U32, "y_codes%d" % c)
+            for g in range(2):
+                y = held([P, 4 * HALF], F32, "y%d%d" % (c, g))
+                for tt in range(2):
+                    acc = psum.tile([P, BANK], F32, name="py", tag="pa" if g == 0 else "pb")
+                    for e in range(2):
+                        u = 4 * g + 2 * tt + e
+                        nc.tensor.matmul_mx(
+                            acc[:, e * HALF:(e + 1) * HALF], lhsT=w3_codes[:, u * P:(u + 1) * P].bitcast(E4M3),
+                            lhsT_scale=w3_planes[:, u * P:(u + 1) * P], rhs=z_codes[c][:].bitcast(E4M3),
+                            rhs_scale=z_planes[c][:], start=True, stop=True,
+                        )
+                    for e in range(2):
+                        t = 2 * tt + e
+                        nc.scalar.activation(
+                            y[:, t * HALF:(t + 1) * HALF], acc[:, e * HALF:(e + 1) * HALF], ACT.Copy,
+                            scale=gain_t[:, 4 * g + t:4 * g + t + 1],
+                        )
+                nc.sync.dma_start(
+                    out_0[512 * g:512 * (g + 1), c * HALF:(c + 1) * HALF].rearrange("(p t) m -> p t m", t=4),
+                    y[:].rearrange("p (t m) -> p t m", t=4),
+                )
+                y_bf = ring.tile([P, 4 * HALF], BF16, name="y_bf", align_bytes=64)
+                nc.vector.tensor_copy(
+                    y_bf[:].rearrange("p (m i t) -> p m t i", i=4, t=4),
+                    y[:].rearrange("p (t m i) -> p m t i", t=4, i=4),
+                )
+                nc.vector.quantize_mx(
+                    y_codes[:, g * HALF:(g + 1) * HALF].bitcast(E4M3),
+                    y_planes[:, g * PAIRS + c * HALF:g * PAIRS + (c + 1) * HALF], y_bf[:],
+                )
+            nc.sync.dma_start(
+                out_1.rearrange("g p m t -> p g (m t)").bitcast(I32)[:, :, c * HALF:(c + 1) * HALF],
+                y_codes[:].bitcast(I32).rearrange("p (g m) -> p g m", g=2),
+            )
+        for d in range(4):
+            queue = nc.sync if d % 2 == 0 else nc.scalar
+            queue.dma_start(
+                out_2[:, 4 * d:4 * d + 4, :].bitcast(I32).rearrange("g r m -> r g m"),
+                y_planes[32 * d:32 * d + 4, :].bitcast(I32).rearrange("r (g m) -> r g m", g=2),
+            )

@@ -20,6 +20,7 @@ P = 128
 PASSES = K // 512
 BANK = 512
 HALF = PAIRS // 2
+SLOT = (0, 2, 1)
 
 
 def tile_list_still_cut_features_kernel(
@@ -29,6 +30,7 @@ def tile_list_still_cut_features_kernel(
     nc = tc.nc
     with ExitStack() as ctx:
         keep = ctx.enter_context(tc.tile_pool(name="keep", bufs=1))
+        shared = ctx.enter_context(tc.tile_pool(name="shared", bufs=1))
         ring = ctx.enter_context(tc.tile_pool(name="ring", bufs=2))
         psum = ctx.enter_context(tc.psum_pool(name="psum", bufs=4))
 
@@ -45,34 +47,37 @@ def tile_list_still_cut_features_kernel(
         def staged(shape, dtype, name, tag):
             return keep.tile(shape, dtype, name=name, tag=tag, align_bytes=64)
 
-        sc_win = staged([P, T], U8, "sc_win", "z")
+        def overlaid(shape, dtype, name, offset):
+            return shared.tile(shape, dtype, name=name, align_bytes=64, offset=offset)
+
+        sc_win = overlaid([P, T], U8, "sc_win", 0)
         nc.gpsimd.memset(sc_win[:].bitcast(I32), 0)
-        v_planes = held([P, PASSES * S], U8, "v_planes")
-        nc.vector.memset(v_planes[:].bitcast(I32), 0)
-        w1_sc_raw = staged([P, PASSES * H], U8, "w1_sc_raw", "small")
-        nc.gpsimd.memset(w1_sc_raw[:].bitcast(I32), 0)
         nc.scalar.dma_start(
             sc_win[0:P:4, :].bitcast(I32), tab_scales[0:2].bitcast(I32).rearrange("a q t -> q a t")
         )
         nc.scalar.dma_start(sc_win[2:P:8, :].bitcast(I32), tab_scales[2].bitcast(I32))
+        warm_in = staged([P, 1], F32, "warm_in", "y")
+        warm_bias = overlaid([P, 1], F32, "warm_bias", T)
+        warm_out = staged([P, 1], F32, "warm_out", "v")
+        nc.gpsimd.memset(warm_in[:], 1.0)
+        nc.gpsimd.memset(warm_bias[:], 0.0)
+        nc.scalar.activation(warm_out[:], warm_in[:], ACT.Sqrt, bias=warm_bias[:])
+        w1_sc_raw = held([P, PASSES * H], U8, "w1_sc_raw")
+        nc.vector.memset(w1_sc_raw[:].bitcast(I32), 0)
+        v_planes = held([P, 4 * S], U8, "v_planes")
+        nc.vector.memset(v_planes[:, 0:PASSES * S].bitcast(I32), 0)
         for d in range(4):
-            nc.gpsimd.dma_start(
+            nc.scalar.dma_start(
                 w1_sc_raw[32 * d:32 * d + 4, :].bitcast(I32).rearrange("r (a c) -> r a c", a=PASSES),
                 w1_scales[:, 4 * d:4 * d + 4, :].bitcast(I32).rearrange("a r c -> r a c"),
             )
-
-        warm = held([P, 1], F32, "warm")
-        warm2 = held([P, 1], F32, "warm2")
-        nc.gpsimd.memset(warm[:], 1.0)
-        nc.scalar.activation(warm2[:], warm[:], ACT.Sqrt)
 
         def load_table(a, tag):
             words = staged([P, T], I32, "tabw%d" % a, tag)
             nc.sync.dma_start(words[:], tab_words[a].rearrange("p t i -> p (t i)").bitcast(I32))
             return words
 
-        def load_w2(a, tag):
-            raw = staged([P, 4 * H], F32, "w2_raw%d" % a, tag)
+        def load_w2(a, raw):
             nc.sync.dma_start(raw[:], w2[512 * a:512 * (a + 1), :].rearrange("(p j) c -> p (j c)", j=4))
             return raw
 
@@ -83,30 +88,36 @@ def tile_list_still_cut_features_kernel(
             w1_words.bitcast(I32).rearrange("a p c -> p a c"),
         )
         tab1 = load_table(1, "y")
+        raw0 = load_w2(0, staged([P, 4 * H], F32, "w2_raw0", "v"))
 
         sc_got = held([P, S], U8, "sc_got")
         nc.vector.tensor_copy(sc_got[:], sc_win[:].indirect(offs_t[:]))
         for d in range(4):
             nc.scalar.dma_start(
-                v_planes[32 * d:32 * d + 4, 0:2 * S].bitcast(I32), sc_got[32 * d:32 * d + 32:4, :].bitcast(I32)
-            )
-        for d in range(4):
-            nc.scalar.dma_start(
-                v_planes[32 * d:32 * d + 4, 2 * S:3 * S].bitcast(I32),
-                sc_got[32 * d + 2:32 * d + 32:8, :].bitcast(I32),
+                v_planes[32 * d:32 * d + 4, :].bitcast(I32), sc_got[32 * d:32 * d + 32:2, :].bitcast(I32)
             )
 
         v_words = [held([P, S], U32, "v_words%d" % a) for a in range(PASSES)]
-        w1_codes = held([P, PASSES * H // 2], I32, "w1_codes")
         w1_planes = held([P, PASSES * H], U8, "w1_planes")
+        w1_codes = []
+
+        def deal_w1(pair, codes):
+            nc.vector.tensor_copy(
+                codes[:].rearrange("p (a t q w) -> p a t q w", a=PASSES, t=2, w=4),
+                w1_raw[:].rearrange("p (a q t w) -> p a t q w", a=PASSES, t=4, w=4)[:, :, 2 * pair:2 * pair + 2],
+            )
+            w1_codes.append(codes)
+
         w2_codes = [held([P, H], U32, "w2_codes%d" % a) for a in range(PASSES)]
         w2_planes = [held([P, H], U8, "w2_planes%d" % a) for a in range(PASSES)]
 
-        def gather_words(a, words):
-            nc.vector.tensor_copy(v_words[a][:], words[:].bitcast(U32).indirect(offs_t[:]))
+        def gather_words(a, words, lo, hi):
+            nc.vector.tensor_copy(
+                v_words[a][:, lo:hi], words[:].bitcast(U32).indirect(offs_t[:, lo // 16:hi // 16])
+            )
 
-        def round_w2(copy, raw, lo, hi):
-            w2_bf = ring.tile([P, (hi - lo) * 512], BF16, name="w2_bf", align_bytes=64)
+        def round_w2(copy, raw, lo, hi, tag):
+            w2_bf = staged([P, (hi - lo) * 512], BF16, "w2_" + tag, tag)
             copy(
                 w2_bf[:].rearrange("p (t q i j) -> p t q j i", q=16, i=8, j=4),
                 raw[:].rearrange("p (j q t i) -> p t q j i", j=4, t=4, i=8)[:, lo:hi],
@@ -118,18 +129,15 @@ def tile_list_still_cut_features_kernel(
                 w2_codes[a][:, lo * P:hi * P].bitcast(E4M3), w2_planes[a][:, lo * P:hi * P], w2_bf[:]
             )
 
-        raw0 = load_w2(0, "z")
-        gather_words(0, tab0)
+        raw1 = load_w2(1, overlaid([P, 4 * H], F32, "w2_raw1", 0))
+        gather_words(0, tab0, 0, S)
         tab2 = load_table(2, "x")
-        nc.vector.tensor_copy(
-            w1_codes[:].rearrange("p (a t q w) -> p a t q w", a=PASSES, t=4, w=4),
-            w1_raw[:].rearrange("p (a q t w) -> p a t q w", a=PASSES, t=4, w=4),
-        )
+        deal_w1(0, held([P, PASSES * H // 4], I32, "w1_codes0"))
         nc.vector.tensor_copy(
             w1_planes[:].bitcast(I32).rearrange("p (a t q w) -> p a t q w", a=PASSES, t=4, w=2),
             w1_sc_raw[:].bitcast(I32).rearrange("p (a q t w) -> p a t q w", a=PASSES, t=4, w=2),
         )
-        small = staged([P, 40], F32, "small", "small")
+        small = held([P, 40], F32, "small")
         with nc.allow_non_contiguous_dma(reason="one value a partition"):
             for t in range(4):
                 nc.gpsimd.dma_start(small[:, 8 * t:8 * t + 1], level.rearrange("(q t i) -> t q i", t=4, i=8)[t])
@@ -137,23 +145,25 @@ def tile_list_still_cut_features_kernel(
         nc.gpsimd.dma_start(
             gain_t.rearrange("p (g t) -> p g t", g=2), rowgain.rearrange("(g p t) -> p g t", g=2, t=4)
         )
-        gather_words(1, tab1)
-        raw1 = load_w2(1, "y")
-        bf0 = round_w2(nc.scalar.copy, raw0, 0, 4)
-        raw2 = load_w2(2, "z")
-        gather_words(2, tab2)
-        allow_t = staged([P, 4 * PAIRS], F32, "allow_t", "x")
+        gather_words(1, tab1, 0, S)
+        bf0 = round_w2(nc.scalar.copy, raw0, 0, 4, "bf0")
+        raw2 = load_w2(2, staged([P, 4 * H], F32, "w2_raw2", "y"))
+        bf1 = round_w2(nc.scalar.copy, raw1, 0, 4, "bf1")
+        allow_t = staged([P, 4 * PAIRS], F32, "allow_t", "v")
         for t in range(4):
             nc.sync.dma_start(
                 allow_t[:, t * PAIRS:(t + 1) * PAIRS], allow.rearrange("(q t i) m -> t q (i m)", t=4, i=8)[t]
             )
         quantise_w2(0, 0, 4, bf0)
-        quantise_w2(1, 0, 4, round_w2(nc.vector.tensor_copy, raw1, 0, 4))
-        w3_raw = staged([P, 4 * N], F32, "w3_raw", "y")
+        gather_words(2, tab2, 0, BANK)
+        gather_words(2, tab2, BANK, S)
+        quantise_w2(1, 0, 4, bf1)
+        quantise_w2(2, 0, 2, round_w2(nc.vector.tensor_copy, raw2, 0, 2, "bf2"))
+        deal_w1(1, staged([P, PASSES * H // 4], I32, "w1_codes1", "bf2"))
+        quantise_w2(2, 2, 4, round_w2(nc.vector.tensor_copy, raw2, 2, 4, "bf3"))
+        w3_raw = overlaid([P, 4 * N], F32, "w3_raw", 0)
         for t in range(4):
             nc.sync.dma_start(w3_raw[:, t * N:(t + 1) * N], w3.rearrange("(q t i) n -> t q (i n)", t=4, i=8)[t])
-        quantise_w2(2, 0, 2, round_w2(nc.vector.tensor_copy, raw2, 0, 2))
-        quantise_w2(2, 2, 4, round_w2(nc.vector.tensor_copy, raw2, 2, 4))
 
         def product(tag, t, half, codes, planes):
             acc = psum.tile([P, BANK], F32, name=tag, tag=tag)
@@ -161,13 +171,14 @@ def tile_list_still_cut_features_kernel(
                 nc.tensor.matmul_mx(
                     acc[:], lhsT=codes(a, t), lhsT_scale=planes(a, t),
                     rhs=v_words[a][:, half * BANK:(half + 1) * BANK].bitcast(E4M3),
-                    rhs_scale=v_planes[:, a * S + half * BANK:a * S + (half + 1) * BANK],
+                    rhs_scale=v_planes[:, SLOT[a] * S + half * BANK:SLOT[a] * S + (half + 1) * BANK],
                     start=(a == 0), stop=(a == PASSES - 1),
                 )
             return acc
 
         def w1c(a, t):
-            return w1_codes[:].bitcast(U8)[:, 2 * (a * H + t * P):2 * (a * H + (t + 1) * P)].bitcast(E2M1)
+            lo = 2 * (2 * a + t % 2) * P
+            return w1_codes[t // 2][:].bitcast(U8)[:, lo:lo + 2 * P].bitcast(E2M1)
 
         def w1p(a, t):
             return w1_planes[:, a * H + t * P:a * H + (t + 1) * P]
@@ -179,100 +190,142 @@ def tile_list_still_cut_features_kernel(
             return w2_planes[a][:, t * P:(t + 1) * P]
 
         root = [held([P, S], F32, "root%d" % t) for t in range(4)]
-        for t in range(4):
-            size = ring.tile([P, S], F32, name="size")
+        h = [held([P, S], F32, "h%d" % t) for t in range(4)]
+        cut1 = [held([P, 4 * HALF], F32, "cut1_0")]
+        cut2 = [held([P, 4 * HALF], F32, "cut2_0")]
+
+        def make_root(t):
             for half in range(2):
+                cols = slice(half * BANK, (half + 1) * BANK)
+                size = ring.tile([P, BANK], F32, name="size")
                 acc = product("pa", t, half, w1c, w1p)
-                nc.scalar.activation(size[:, half * BANK:(half + 1) * BANK], acc[:], ACT.Abs)
-            nc.scalar.activation(root[t][:], size[:], ACT.Sqrt, bias=small[:, 8 * t:8 * t + 1])
+                nc.scalar.activation(size[:], acc[:], ACT.Abs)
+                nc.scalar.activation(root[t][:, cols], size[:], ACT.Sqrt, bias=small[:, 8 * t:8 * t + 1])
 
-        cut1 = held([P, 4 * PAIRS], F32, "cut1")
-        cut2 = held([P, 4 * PAIRS], F32, "cut2")
+        def make_h(t):
+            for half in range(2):
+                cols = slice(half * BANK, (half + 1) * BANK)
+                acc = product("pb", t, half, w2c, w2p)
+                nc.vector.tensor_tensor(h[t][:, cols], acc[:], root[t][:, cols], ALU.add)
 
-        def pick(h, t, lo, hi):
+        def pick(t, c):
+            lo, hi = c * HALF, (c + 1) * HALF
+            place = slice(t * HALF, (t + 1) * HALF)
             nc.vector.tensor_tensor(
-                cut1[:, t * PAIRS + lo:t * PAIRS + hi], h[:].indirect(pos1_t[:, lo // 16:hi // 16]),
+                cut1[c][:, place], h[t][:].indirect(pos1_t[:, lo // 16:hi // 16]),
                 allow_t[:, t * PAIRS + lo:t * PAIRS + hi], ALU.add,
             )
-            nc.vector.tensor_copy(
-                cut2[:, t * PAIRS + lo:t * PAIRS + hi], h[:].indirect(pos2_t[:, lo // 16:hi // 16])
-            )
+            nc.vector.tensor_copy(cut2[c][:, place], h[t][:].indirect(pos2_t[:, lo // 16:hi // 16]))
 
-        h_last = None
+        make_root(0)
+        make_root(1)
         for t in range(4):
-            h = ring.tile([P, S], F32, name="h")
-            for half in range(2):
-                acc = product("pb", t, half, w2c, w2p)
-                cols = slice(half * BANK, (half + 1) * BANK)
-                nc.vector.tensor_tensor(h[:, cols], acc[:], root[t][:, cols], ALU.add)
-            if t < 3:
-                pick(h, t, 0, PAIRS)
-            h_last = h
+            if t in (1, 2):
+                make_root(t + 1)
+            make_h(t)
+            pick(t, 0)
 
-        w3_bf = held([P, 4 * N], BF16, "w3_bf")
         w3_codes = held([P, N], U32, "w3_codes")
         w3_planes = held([P, N], U8, "w3_planes")
         for g in range(2):
+            w3_bf = staged([P, 2048], BF16, "w3_bf%d" % g, "late%d" % g)
             nc.scalar.copy(
-                w3_bf[:, g * 2048:(g + 1) * 2048].rearrange("p (t m j) -> p m j t", t=4, j=4),
+                w3_bf[:].rearrange("p (t m j) -> p m j t", t=4, j=4),
                 w3_raw[:].rearrange("p (j g m t) -> p g m j t", j=4, g=2, t=4)[:, g],
             )
             nc.vector.quantize_mx(
                 w3_codes[:, g * 512:(g + 1) * 512].bitcast(E4M3), w3_planes[:, g * 512:(g + 1) * 512],
-                w3_bf[:, g * 2048:(g + 1) * 2048],
+                w3_bf[:],
             )
 
-        z_codes = []
-        z_planes = []
-        for c in range(2):
-            pick(h_last, 3, c * HALF, (c + 1) * HALF)
+        cut1.append(staged([P, 4 * HALF], F32, "cut1_1", "late0"))
+        cut2.append(staged([P, 4 * HALF], F32, "cut2_1", "late1"))
+
+        y_planes = held([P, 2 * PAIRS], U8, "y_planes")
+
+        def make_z(c):
             z_bf = ring.tile([P, 4 * HALF], BF16, name="z_bf", align_bytes=64)
-            view1 = cut1[:].rearrange("p (t c m i) -> p c m t i", t=4, c=2, i=4)[:, c]
-            view2 = cut2[:].rearrange("p (t c m i) -> p c m t i", t=4, c=2, i=4)[:, c]
-            nc.vector.tensor_tensor(z_bf[:].rearrange("p (m i t) -> p m t i", i=4, t=4), view1, view2, ALU.min)
+            nc.vector.tensor_tensor(
+                z_bf[:].rearrange("p (m i t) -> p m t i", i=4, t=4),
+                cut1[c][:].rearrange("p (t m i) -> p m t i", t=4, i=4),
+                cut2[c][:].rearrange("p (t m i) -> p m t i", t=4, i=4),
+                ALU.min,
+            )
+            return z_bf
+
+        def quantise_z(c, z_bf):
             zc = held([P, HALF], U32, "z_codes%d" % c)
             zp = held([P, HALF], U8, "z_planes%d" % c)
             nc.vector.quantize_mx(zc[:].bitcast(E4M3), zp[:], z_bf[:])
-            z_codes.append(zc)
-            z_planes.append(zp)
+            return zc, zp
 
-        y_planes = held([P, 2 * PAIRS], U8, "y_planes")
-        for c in range(2):
-            y_codes = held([P, 2 * HALF], U32, "y_codes%d" % c)
-            for g in range(2):
-                y = held([P, 4 * HALF], F32, "y%d%d" % (c, g))
-                for tt in range(2):
-                    acc = psum.tile([P, BANK], F32, name="py", tag="pa" if g == 0 else "pb")
-                    for e in range(2):
-                        u = 4 * g + 2 * tt + e
-                        nc.tensor.matmul_mx(
-                            acc[:, e * HALF:(e + 1) * HALF], lhsT=w3_codes[:, u * P:(u + 1) * P].bitcast(E4M3),
-                            lhsT_scale=w3_planes[:, u * P:(u + 1) * P], rhs=z_codes[c][:].bitcast(E4M3),
-                            rhs_scale=z_planes[c][:], start=True, stop=True,
+        def make_y(c, g, z, on_vector):
+            y = held([P, 4 * HALF], F32, "y%d%d" % (c, g))
+            for tt in range(2):
+                acc = psum.tile([P, BANK], F32, name="py", tag="pa" if g == 0 else "pb")
+                for e in range(2):
+                    u = 4 * g + 2 * tt + e
+                    nc.tensor.matmul_mx(
+                        acc[:, e * HALF:(e + 1) * HALF], lhsT=w3_codes[:, u * P:(u + 1) * P].bitcast(E4M3),
+                        lhsT_scale=w3_planes[:, u * P:(u + 1) * P], rhs=z[0][:].bitcast(E4M3),
+                        rhs_scale=z[1][:], start=True, stop=True,
+                    )
+                for e in range(2):
+                    t = 2 * tt + e
+                    gain = gain_t[:, 4 * g + t:4 * g + t + 1]
+                    if on_vector:
+                        nc.vector.tensor_scalar(
+                            y[:, t * HALF:(t + 1) * HALF], acc[:, e * HALF:(e + 1) * HALF], gain, None, ALU.mult
                         )
-                    for e in range(2):
-                        t = 2 * tt + e
+                    else:
                         nc.scalar.activation(
-                            y[:, t * HALF:(t + 1) * HALF], acc[:, e * HALF:(e + 1) * HALF], ACT.Copy,
-                            scale=gain_t[:, 4 * g + t:4 * g + t + 1],
+                            y[:, t * HALF:(t + 1) * HALF], acc[:, e * HALF:(e + 1) * HALF], ACT.Copy, scale=gain
                         )
-                nc.sync.dma_start(
-                    out_0[512 * g:512 * (g + 1), c * HALF:(c + 1) * HALF].rearrange("(p t) m -> p t m", t=4),
-                    y[:].rearrange("p (t m) -> p t m", t=4),
-                )
-                y_bf = ring.tile([P, 4 * HALF], BF16, name="y_bf", align_bytes=64)
-                nc.vector.tensor_copy(
-                    y_bf[:].rearrange("p (m i t) -> p m t i", i=4, t=4),
-                    y[:].rearrange("p (t m i) -> p m t i", t=4, i=4),
-                )
-                nc.vector.quantize_mx(
-                    y_codes[:, g * HALF:(g + 1) * HALF].bitcast(E4M3),
-                    y_planes[:, g * PAIRS + c * HALF:g * PAIRS + (c + 1) * HALF], y_bf[:],
-                )
+            nc.sync.dma_start(
+                out_0[512 * g:512 * (g + 1), c * HALF:(c + 1) * HALF].rearrange("(p t) m -> p t m", t=4),
+                y[:].rearrange("p (t m) -> p t m", t=4),
+            )
+            return y
+
+        def round_y(copy, y):
+            y_bf = ring.tile([P, 4 * HALF], BF16, name="y_bf", align_bytes=64, bufs=4)
+            copy(
+                y_bf[:].rearrange("p (m i t) -> p m t i", i=4, t=4),
+                y[:].rearrange("p (t m i) -> p m t i", t=4, i=4),
+            )
+            return y_bf
+
+        def quantise_y(c, g, y_bf, y_codes):
+            nc.vector.quantize_mx(
+                y_codes[:, g * HALF:(g + 1) * HALF].bitcast(E4M3),
+                y_planes[:, g * PAIRS + c * HALF:g * PAIRS + (c + 1) * HALF], y_bf[:],
+            )
+
+        def store_codes(c, y_codes):
             nc.sync.dma_start(
                 out_1.rearrange("g p m t -> p g (m t)").bitcast(I32)[:, :, c * HALF:(c + 1) * HALF],
                 y_codes[:].bitcast(I32).rearrange("p (g m) -> p g m", g=2),
             )
+
+        y_codes = [held([P, 2 * HALF], U32, "y_codes%d" % c) for c in range(2)]
+        z_bf0 = make_z(0)
+        pick(0, 1)
+        z0 = quantise_z(0, z_bf0)
+        y0 = [make_y(0, g, z0, False) for g in range(2)]
+        y_bf0 = [round_y(nc.scalar.copy, y0[g]) for g in range(2)]
+        for t in range(1, 4):
+            pick(t, 1)
+        z1 = quantise_z(1, make_z(1))
+        for g in range(2):
+            quantise_y(0, g, y_bf0[g], y_codes[0])
+        store_codes(0, y_codes[0])
+        y11 = make_y(1, 1, z1, True)
+        y10 = make_y(1, 0, z1, False)
+        y_bf11 = round_y(nc.vector.tensor_copy, y11)
+        y_bf10 = round_y(nc.scalar.copy, y10)
+        quantise_y(1, 1, y_bf11, y_codes[1])
+        quantise_y(1, 0, y_bf10, y_codes[1])
+        store_codes(1, y_codes[1])
         for d in range(4):
             queue = nc.sync if d % 2 == 0 else nc.scalar
             queue.dma_start(

@@ -17,10 +17,15 @@ ACT = mybir.ActivationFunctionType
 ALU = mybir.AluOpType
 
 P = 128
-PASSES = K // 512
+PACK = 4
+K_PASS = P * PACK
+PASSES = K // K_PASS
 BANK = 512
-HALF = PAIRS // 2
-SLOT = (0, 2, 1)
+QUADS = 4
+SWEEP = PAIRS // 2
+LIST_ROWS = 16
+
+PLANE_OF_PASS = (0, 2, 1)
 
 
 def tile_list_still_cut_features_kernel(
@@ -37,298 +42,314 @@ def tile_list_still_cut_features_kernel(
         def held(shape, dtype, name):
             return keep.tile(shape, dtype, name=name, align_bytes=64)
 
-        offs_t = keep.tile([P, S // 16], U16, name="offs_t")
-        pos1_t = keep.tile([P, PAIRS // 16], U16, name="pos1_t")
-        pos2_t = keep.tile([P, PAIRS // 16], U16, name="pos2_t")
+        def after(tag, shape, dtype, name):
+            return keep.tile(shape, dtype, name=name, tag=tag, align_bytes=64)
+
+        def overlaid(offset, shape, dtype, name):
+            return shared.tile(shape, dtype, name=name, align_bytes=64, offset=offset)
+
+        offs_t = keep.tile([P, S // LIST_ROWS], U16, name="offs_t")
+        pos1_t = keep.tile([P, PAIRS // LIST_ROWS], U16, name="pos1_t")
+        pos2_t = keep.tile([P, PAIRS // LIST_ROWS], U16, name="pos2_t")
         nc.sync.dma_start(offs_t[:], offs)
         nc.sync.dma_start(pos1_t[:], pos1)
         nc.sync.dma_start(pos2_t[:], pos2)
 
-        def staged(shape, dtype, name, tag):
-            return keep.tile(shape, dtype, name=name, tag=tag, align_bytes=64)
-
-        def overlaid(shape, dtype, name, offset):
-            return shared.tile(shape, dtype, name=name, align_bytes=64, offset=offset)
-
-        sc_win = overlaid([P, T], U8, "sc_win", 0)
-        nc.gpsimd.memset(sc_win[:].bitcast(I32), 0)
+        scale_window = overlaid(0, [P, T], U8, "scale_window")
+        nc.gpsimd.memset(scale_window[:].bitcast(I32), 0)
         nc.scalar.dma_start(
-            sc_win[0:P:4, :].bitcast(I32), tab_scales[0:2].bitcast(I32).rearrange("a q t -> q a t")
+            scale_window[0:P:4, :].bitcast(I32), tab_scales[0:2].bitcast(I32).rearrange("a q t -> q a t")
         )
-        nc.scalar.dma_start(sc_win[2:P:8, :].bitcast(I32), tab_scales[2].bitcast(I32))
-        warm_in = staged([P, 1], F32, "warm_in", "y")
-        warm_bias = overlaid([P, 1], F32, "warm_bias", T)
-        warm_out = staged([P, 1], F32, "warm_out", "v")
+        nc.scalar.dma_start(scale_window[2:P:8, :].bitcast(I32), tab_scales[2].bitcast(I32))
+
+        warm_in = after("table_odd", [P, 1], F32, "warm_in")
+        warm_bias = overlaid(T, [P, 1], F32, "warm_bias")
+        warm_out = after("w2_first", [P, 1], F32, "warm_out")
         nc.gpsimd.memset(warm_in[:], 1.0)
         nc.gpsimd.memset(warm_bias[:], 0.0)
         nc.scalar.activation(warm_out[:], warm_in[:], ACT.Sqrt, bias=warm_bias[:])
-        w1_sc_raw = held([P, PASSES * H], U8, "w1_sc_raw")
-        nc.vector.memset(w1_sc_raw[:].bitcast(I32), 0)
+
+        w1_planes_raw = held([P, PASSES * H], U8, "w1_planes_raw")
+        nc.vector.memset(w1_planes_raw[:].bitcast(I32), 0)
         v_planes = held([P, 4 * S], U8, "v_planes")
         nc.vector.memset(v_planes[:, 0:PASSES * S].bitcast(I32), 0)
-        for d in range(4):
+        for d in range(QUADS):
             nc.scalar.dma_start(
-                w1_sc_raw[32 * d:32 * d + 4, :].bitcast(I32).rearrange("r (a c) -> r a c", a=PASSES),
+                w1_planes_raw[32 * d:32 * d + 4, :].bitcast(I32).rearrange("r (a c) -> r a c", a=PASSES),
                 w1_scales[:, 4 * d:4 * d + 4, :].bitcast(I32).rearrange("a r c -> r a c"),
             )
 
-        def load_table(a, tag):
-            words = staged([P, T], I32, "tabw%d" % a, tag)
+        def load_table(a, words):
             nc.sync.dma_start(words[:], tab_words[a].rearrange("p t i -> p (t i)").bitcast(I32))
             return words
 
         def load_w2(a, raw):
-            nc.sync.dma_start(raw[:], w2[512 * a:512 * (a + 1), :].rearrange("(p j) c -> p (j c)", j=4))
+            nc.sync.dma_start(raw[:], w2[K_PASS * a:K_PASS * (a + 1), :].rearrange("(p j) c -> p (j c)", j=PACK))
             return raw
 
-        tab0 = load_table(0, "x")
+        tab0 = load_table(0, after("table_even", [P, T], I32, "tab0"))
         w1_raw = held([P, PASSES * H // 2], I32, "w1_raw")
         nc.sync.dma_start(
             w1_raw[:].rearrange("p (a c) -> p a c", a=PASSES),
             w1_words.bitcast(I32).rearrange("a p c -> p a c"),
         )
-        tab1 = load_table(1, "y")
-        raw0 = load_w2(0, staged([P, 4 * H], F32, "w2_raw0", "v"))
+        tab1 = load_table(1, after("table_odd", [P, T], I32, "tab1"))
+        w2_raw0 = load_w2(0, after("w2_first", [P, PACK * H], F32, "w2_raw0"))
 
-        sc_got = held([P, S], U8, "sc_got")
-        nc.vector.tensor_copy(sc_got[:], sc_win[:].indirect(offs_t[:]))
-        for d in range(4):
+        scales_got = held([P, S], U8, "scales_got")
+        nc.vector.tensor_copy(scales_got[:], scale_window[:].indirect(offs_t[:]))
+        for d in range(QUADS):
             nc.scalar.dma_start(
-                v_planes[32 * d:32 * d + 4, :].bitcast(I32), sc_got[32 * d:32 * d + 32:2, :].bitcast(I32)
+                v_planes[32 * d:32 * d + 4, :].bitcast(I32), scales_got[32 * d:32 * d + 32:2, :].bitcast(I32)
             )
 
         v_words = [held([P, S], U32, "v_words%d" % a) for a in range(PASSES)]
-        w1_planes = held([P, PASSES * H], U8, "w1_planes")
         w1_codes = []
-
-        def deal_w1(pair, codes):
-            nc.vector.tensor_copy(
-                codes[:].rearrange("p (a t q w) -> p a t q w", a=PASSES, t=2, w=4),
-                w1_raw[:].rearrange("p (a q t w) -> p a t q w", a=PASSES, t=4, w=4)[:, :, 2 * pair:2 * pair + 2],
-            )
-            w1_codes.append(codes)
-
         w2_codes = [held([P, H], U32, "w2_codes%d" % a) for a in range(PASSES)]
         w2_planes = [held([P, H], U8, "w2_planes%d" % a) for a in range(PASSES)]
 
         def gather_words(a, words, lo, hi):
             nc.vector.tensor_copy(
-                v_words[a][:, lo:hi], words[:].bitcast(U32).indirect(offs_t[:, lo // 16:hi // 16])
+                v_words[a][:, lo:hi], words[:].bitcast(U32).indirect(offs_t[:, lo // LIST_ROWS:hi // LIST_ROWS])
             )
 
-        def round_w2(copy, raw, lo, hi, tag):
-            w2_bf = staged([P, (hi - lo) * 512], BF16, "w2_" + tag, tag)
-            copy(
-                w2_bf[:].rearrange("p (t q i j) -> p t q j i", q=16, i=8, j=4),
-                raw[:].rearrange("p (j q t i) -> p t q j i", j=4, t=4, i=8)[:, lo:hi],
+        def deal_w1(pair, codes):
+            nc.vector.tensor_copy(
+                codes[:].rearrange("p (a t q w) -> p a t q w", a=PASSES, t=2, w=4),
+                w1_raw[:].rearrange("p (a q t w) -> p a t q w", a=PASSES, t=PACK, w=4)[:, :, 2 * pair:2 * pair + 2],
+            )
+            w1_codes.append(codes)
+
+        def round_pass_on_scalar(raw, w2_bf):
+            nc.scalar.copy(
+                w2_bf[:].rearrange("p (t q i j) -> p t q j i", q=16, i=8, j=PACK),
+                raw[:].rearrange("p (j q t i) -> p t q j i", j=PACK, t=PACK, i=8),
             )
             return w2_bf
+
+        def round_tile_on_vector(raw, t, w2_bf):
+            nc.vector.tensor_copy(
+                w2_bf.rearrange("p (q e i j) -> p q e j i", e=2, i=4, j=PACK),
+                raw[:].rearrange("p (j q t e i) -> p t q e j i", j=PACK, t=PACK, e=2, i=4)[:, t],
+            )
 
         def quantise_w2(a, lo, hi, w2_bf):
             nc.vector.quantize_mx(
                 w2_codes[a][:, lo * P:hi * P].bitcast(E4M3), w2_planes[a][:, lo * P:hi * P], w2_bf[:]
             )
 
-        raw1 = load_w2(1, overlaid([P, 4 * H], F32, "w2_raw1", 0))
+        tab2 = load_table(2, overlaid(0, [P, T], I32, "tab2"))
         gather_words(0, tab0, 0, S)
-        tab2 = load_table(2, "x")
+        w2_raw1 = load_w2(1, after("table_even", [P, PACK * H], F32, "w2_raw1"))
         deal_w1(0, held([P, PASSES * H // 4], I32, "w1_codes0"))
+        w1_planes = held([P, PASSES * H], U8, "w1_planes")
         nc.vector.tensor_copy(
-            w1_planes[:].bitcast(I32).rearrange("p (a t q w) -> p a t q w", a=PASSES, t=4, w=2),
-            w1_sc_raw[:].bitcast(I32).rearrange("p (a q t w) -> p a t q w", a=PASSES, t=4, w=2),
+            w1_planes[:].bitcast(I32).rearrange("p (a t q w) -> p a t q w", a=PASSES, t=PACK, w=2),
+            w1_planes_raw[:].bitcast(I32).rearrange("p (a q t w) -> p a t q w", a=PASSES, t=PACK, w=2),
         )
-        small = held([P, 40], F32, "small")
+
+        row_constants = held([P, 40], F32, "row_constants")
         with nc.allow_non_contiguous_dma(reason="one value a partition"):
-            for t in range(4):
-                nc.gpsimd.dma_start(small[:, 8 * t:8 * t + 1], level.rearrange("(q t i) -> t q i", t=4, i=8)[t])
-        gain_t = small[:, 32:40]
+            for t in range(PACK):
+                nc.gpsimd.dma_start(
+                    row_constants[:, 8 * t:8 * t + 1], level.rearrange("(q t i) -> t q i", t=PACK, i=8)[t]
+                )
+        gains = row_constants[:, 32:40]
         nc.gpsimd.dma_start(
-            gain_t.rearrange("p (g t) -> p g t", g=2), rowgain.rearrange("(g p t) -> p g t", g=2, t=4)
+            gains.rearrange("p (g t) -> p g t", g=2), rowgain.rearrange("(g p t) -> p g t", g=2, t=PACK)
         )
+
         gather_words(1, tab1, 0, S)
-        bf0 = round_w2(nc.scalar.copy, raw0, 0, 4, "bf0")
-        raw2 = load_w2(2, staged([P, 4 * H], F32, "w2_raw2", "y"))
-        bf1 = round_w2(nc.scalar.copy, raw1, 0, 4, "bf1")
-        allow_t = staged([P, 4 * PAIRS], F32, "allow_t", "v")
-        for t in range(4):
+
+        w2_bf0 = round_pass_on_scalar(w2_raw0, held([P, PACK * H], BF16, "w2_bf0"))
+        w2_raw2 = load_w2(2, after("table_odd", [P, PACK * H], F32, "w2_raw2"))
+        allow_t = after("w2_first", [P, PACK * PAIRS], F32, "allow_t")
+        for t in range(PACK):
             nc.sync.dma_start(
-                allow_t[:, t * PAIRS:(t + 1) * PAIRS], allow.rearrange("(q t i) m -> t q (i m)", t=4, i=8)[t]
+                allow_t[:, t * PAIRS:(t + 1) * PAIRS], allow.rearrange("(q t i) m -> t q (i m)", t=PACK, i=8)[t]
             )
-        quantise_w2(0, 0, 4, bf0)
         gather_words(2, tab2, 0, BANK)
         gather_words(2, tab2, BANK, S)
-        quantise_w2(1, 0, 4, bf1)
-        quantise_w2(2, 0, 2, round_w2(nc.vector.tensor_copy, raw2, 0, 2, "bf2"))
-        deal_w1(1, staged([P, PASSES * H // 4], I32, "w1_codes1", "bf2"))
-        quantise_w2(2, 2, 4, round_w2(nc.vector.tensor_copy, raw2, 2, 4, "bf3"))
-        w3_raw = overlaid([P, 4 * N], F32, "w3_raw", 0)
-        for t in range(4):
-            nc.sync.dma_start(w3_raw[:, t * N:(t + 1) * N], w3.rearrange("(q t i) n -> t q (i n)", t=4, i=8)[t])
+        w2_bf1 = held([P, PACK * H], BF16, "w2_bf1")
+        for t in range(PACK):
+            round_tile_on_vector(w2_raw1, t, w2_bf1[:, t * K_PASS:(t + 1) * K_PASS])
+        quantise_w2(0, 0, PACK, w2_bf0)
+        quantise_w2(1, 0, PACK, w2_bf1)
+        last_bf0 = held([P, K_PASS], BF16, "last_bf0")
+        last_bf1 = after("w2_last", [P, K_PASS], BF16, "last_bf1")
+        last_bf23 = held([P, 2 * K_PASS], BF16, "last_bf23")
+        round_tile_on_vector(w2_raw2, 0, last_bf0[:])
+        round_tile_on_vector(w2_raw2, 1, last_bf1[:])
+        quantise_w2(2, 0, 1, last_bf0)
+        quantise_w2(2, 1, 2, last_bf1)
+        deal_w1(1, after("w2_last", [P, PASSES * H // 4], I32, "w1_codes1"))
+        round_tile_on_vector(w2_raw2, 2, last_bf23[:, 0:K_PASS])
+        round_tile_on_vector(w2_raw2, 3, last_bf23[:, K_PASS:2 * K_PASS])
+        quantise_w2(2, 2, PACK, last_bf23)
+        w3_raw = after("table_even", [P, PACK * N], F32, "w3_raw")
+        for t in range(PACK):
+            nc.sync.dma_start(w3_raw[:, t * N:(t + 1) * N], w3.rearrange("(q t i) n -> t q (i n)", t=PACK, i=8)[t])
 
-        def product(tag, t, half, codes, planes):
+        def product(tag, half, weight):
             acc = psum.tile([P, BANK], F32, name=tag, tag=tag)
             for a in range(PASSES):
+                codes, plane = weight(a)
+                plane_lo = PLANE_OF_PASS[a] * S + half * BANK
                 nc.tensor.matmul_mx(
-                    acc[:], lhsT=codes(a, t), lhsT_scale=planes(a, t),
+                    acc[:], lhsT=codes, lhsT_scale=plane,
                     rhs=v_words[a][:, half * BANK:(half + 1) * BANK].bitcast(E4M3),
-                    rhs_scale=v_planes[:, SLOT[a] * S + half * BANK:SLOT[a] * S + (half + 1) * BANK],
+                    rhs_scale=v_planes[:, plane_lo:plane_lo + BANK],
                     start=(a == 0), stop=(a == PASSES - 1),
                 )
             return acc
 
-        def w1c(a, t):
-            lo = 2 * (2 * a + t % 2) * P
-            return w1_codes[t // 2][:].bitcast(U8)[:, lo:lo + 2 * P].bitcast(E2M1)
+        root = [held([P, S], F32, "root%d" % t) for t in range(PACK)]
+        h = [held([P, S], F32, "h%d" % t) for t in range(PACK)]
+        cut1 = [held([P, PACK * SWEEP], F32, "cut1_0")]
+        cut2 = [held([P, PACK * SWEEP], F32, "cut2_0")]
 
-        def w1p(a, t):
-            return w1_planes[:, a * H + t * P:a * H + (t + 1) * P]
+        def make_root(t, width):
+            def w1_operand(a):
+                lo = 2 * (2 * a + t % 2) * P
+                codes = w1_codes[t // 2][:].bitcast(U8)[:, lo:lo + 2 * P].bitcast(E2M1)
+                return codes, w1_planes[:, a * H + t * P:a * H + (t + 1) * P]
 
-        def w2c(a, t):
-            return w2_codes[a][:, t * P:(t + 1) * P].bitcast(E4M3)
-
-        def w2p(a, t):
-            return w2_planes[a][:, t * P:(t + 1) * P]
-
-        root = [held([P, S], F32, "root%d" % t) for t in range(4)]
-        h = [held([P, S], F32, "h%d" % t) for t in range(4)]
-        cut1 = [held([P, 4 * HALF], F32, "cut1_0")]
-        cut2 = [held([P, 4 * HALF], F32, "cut2_0")]
-
-        def make_root(t):
+            size = ring.tile([P, S], F32, name="size")
             for half in range(2):
-                cols = slice(half * BANK, (half + 1) * BANK)
-                size = ring.tile([P, BANK], F32, name="size")
-                acc = product("pa", t, half, w1c, w1p)
-                nc.scalar.activation(size[:], acc[:], ACT.Abs)
-                nc.scalar.activation(root[t][:, cols], size[:], ACT.Sqrt, bias=small[:, 8 * t:8 * t + 1])
+                hi = (half + 1) * BANK
+                nc.scalar.activation(size[:, hi - BANK:hi], product("w1_sum", half, w1_operand)[:], ACT.Abs)
+                if hi % width == 0:
+                    nc.scalar.activation(
+                        root[t][:, hi - width:hi], size[:, hi - width:hi], ACT.Sqrt,
+                        bias=row_constants[:, 8 * t:8 * t + 1],
+                    )
 
         def make_h(t):
+            def w2_operand(a):
+                return w2_codes[a][:, t * P:(t + 1) * P].bitcast(E4M3), w2_planes[a][:, t * P:(t + 1) * P]
+
             for half in range(2):
                 cols = slice(half * BANK, (half + 1) * BANK)
-                acc = product("pb", t, half, w2c, w2p)
-                nc.vector.tensor_tensor(h[t][:, cols], acc[:], root[t][:, cols], ALU.add)
+                nc.vector.tensor_tensor(h[t][:, cols], product("w2_sum", half, w2_operand)[:], root[t][:, cols], ALU.add)
 
         def pick(t, c):
-            lo, hi = c * HALF, (c + 1) * HALF
-            place = slice(t * HALF, (t + 1) * HALF)
+            lo, hi = c * SWEEP, (c + 1) * SWEEP
+            place = slice(t * SWEEP, (t + 1) * SWEEP)
             nc.vector.tensor_tensor(
-                cut1[c][:, place], h[t][:].indirect(pos1_t[:, lo // 16:hi // 16]),
+                cut1[c][:, place], h[t][:].indirect(pos1_t[:, lo // LIST_ROWS:hi // LIST_ROWS]),
                 allow_t[:, t * PAIRS + lo:t * PAIRS + hi], ALU.add,
             )
-            nc.vector.tensor_copy(cut2[c][:, place], h[t][:].indirect(pos2_t[:, lo // 16:hi // 16]))
+            nc.vector.tensor_copy(cut2[c][:, place], h[t][:].indirect(pos2_t[:, lo // LIST_ROWS:hi // LIST_ROWS]))
 
-        make_root(0)
-        make_root(1)
-        for t in range(4):
-            if t in (1, 2):
-                make_root(t + 1)
+        make_root(0, BANK)
+        make_root(1, S)
+        for t in range(PACK):
+            if 0 < t < PACK - 1:
+                make_root(t + 1, S)
             make_h(t)
             pick(t, 0)
 
         w3_codes = held([P, N], U32, "w3_codes")
         w3_planes = held([P, N], U8, "w3_planes")
         for g in range(2):
-            w3_bf = staged([P, 2048], BF16, "w3_bf%d" % g, "late%d" % g)
+            w3_bf = after("w3_bf%d" % g, [P, PACK * K_PASS], BF16, "w3_bf%d" % g)
             nc.scalar.copy(
-                w3_bf[:].rearrange("p (t m j) -> p m j t", t=4, j=4),
-                w3_raw[:].rearrange("p (j g m t) -> p g m j t", j=4, g=2, t=4)[:, g],
+                w3_bf[:].rearrange("p (t m j) -> p m j t", t=PACK, j=PACK),
+                w3_raw[:].rearrange("p (j g m t) -> p g m j t", j=PACK, g=2, t=PACK)[:, g],
             )
-            nc.vector.quantize_mx(
-                w3_codes[:, g * 512:(g + 1) * 512].bitcast(E4M3), w3_planes[:, g * 512:(g + 1) * 512],
-                w3_bf[:],
-            )
+            cols = slice(g * K_PASS, (g + 1) * K_PASS)
+            nc.vector.quantize_mx(w3_codes[:, cols].bitcast(E4M3), w3_planes[:, cols], w3_bf[:])
 
-        cut1.append(staged([P, 4 * HALF], F32, "cut1_1", "late0"))
-        cut2.append(staged([P, 4 * HALF], F32, "cut2_1", "late1"))
+        cut1.append(after("w3_bf0", [P, PACK * SWEEP], F32, "cut1_1"))
+        cut2.append(after("w3_bf1", [P, PACK * SWEEP], F32, "cut2_1"))
 
-        y_planes = held([P, 2 * PAIRS], U8, "y_planes")
+        def by_four(ap):
+            return ap.rearrange("p (t m i) -> p m t i", t=PACK, i=4)
+
+        def as_words(ap):
+            return ap.rearrange("p (m i t) -> p m t i", i=4, t=PACK)
 
         def make_z(c):
-            z_bf = ring.tile([P, 4 * HALF], BF16, name="z_bf", align_bytes=64)
-            nc.vector.tensor_tensor(
-                z_bf[:].rearrange("p (m i t) -> p m t i", i=4, t=4),
-                cut1[c][:].rearrange("p (t m i) -> p m t i", t=4, i=4),
-                cut2[c][:].rearrange("p (t m i) -> p m t i", t=4, i=4),
-                ALU.min,
-            )
+            z_bf = ring.tile([P, PACK * SWEEP], BF16, name="z_bf", align_bytes=64)
+            nc.vector.tensor_tensor(as_words(z_bf[:]), by_four(cut1[c][:]), by_four(cut2[c][:]), ALU.min)
             return z_bf
 
         def quantise_z(c, z_bf):
-            zc = held([P, HALF], U32, "z_codes%d" % c)
-            zp = held([P, HALF], U8, "z_planes%d" % c)
-            nc.vector.quantize_mx(zc[:].bitcast(E4M3), zp[:], z_bf[:])
-            return zc, zp
+            z_codes = held([P, SWEEP], U32, "z_codes%d" % c)
+            z_plane = held([P, SWEEP], U8, "z_plane%d" % c)
+            nc.vector.quantize_mx(z_codes[:].bitcast(E4M3), z_plane[:], z_bf[:])
+            return z_codes, z_plane
 
-        def make_y(c, g, z, on_vector):
-            y = held([P, 4 * HALF], F32, "y%d%d" % (c, g))
-            for tt in range(2):
-                acc = psum.tile([P, BANK], F32, name="py", tag="pa" if g == 0 else "pb")
-                for e in range(2):
-                    u = 4 * g + 2 * tt + e
+        def gain_on_scalar(out, acc, gain):
+            nc.scalar.activation(out, acc, ACT.Copy, scale=gain)
+
+        def gain_on_vector(out, acc, gain):
+            nc.vector.tensor_scalar(out, acc, gain, None, ALU.mult)
+
+        def make_y(c, g, z, apply_gain):
+            z_codes, z_plane = z
+            y = held([P, PACK * SWEEP], F32, "y%d%d" % (c, g))
+            for bank in range(2):
+                acc = psum.tile([P, BANK], F32, name="y_sum", tag=("w1_sum", "w2_sum")[g])
+                for side in range(2):
+                    u = PACK * g + 2 * bank + side
                     nc.tensor.matmul_mx(
-                        acc[:, e * HALF:(e + 1) * HALF], lhsT=w3_codes[:, u * P:(u + 1) * P].bitcast(E4M3),
-                        lhsT_scale=w3_planes[:, u * P:(u + 1) * P], rhs=z[0][:].bitcast(E4M3),
-                        rhs_scale=z[1][:], start=True, stop=True,
+                        acc[:, side * SWEEP:(side + 1) * SWEEP],
+                        lhsT=w3_codes[:, u * P:(u + 1) * P].bitcast(E4M3), lhsT_scale=w3_planes[:, u * P:(u + 1) * P],
+                        rhs=z_codes[:].bitcast(E4M3), rhs_scale=z_plane[:], start=True, stop=True,
                     )
-                for e in range(2):
-                    t = 2 * tt + e
-                    gain = gain_t[:, 4 * g + t:4 * g + t + 1]
-                    if on_vector:
-                        nc.vector.tensor_scalar(
-                            y[:, t * HALF:(t + 1) * HALF], acc[:, e * HALF:(e + 1) * HALF], gain, None, ALU.mult
-                        )
-                    else:
-                        nc.scalar.activation(
-                            y[:, t * HALF:(t + 1) * HALF], acc[:, e * HALF:(e + 1) * HALF], ACT.Copy, scale=gain
-                        )
+                for side in range(2):
+                    t = 2 * bank + side
+                    apply_gain(
+                        y[:, t * SWEEP:(t + 1) * SWEEP], acc[:, side * SWEEP:(side + 1) * SWEEP],
+                        gains[:, PACK * g + t:PACK * g + t + 1],
+                    )
             nc.sync.dma_start(
-                out_0[512 * g:512 * (g + 1), c * HALF:(c + 1) * HALF].rearrange("(p t) m -> p t m", t=4),
-                y[:].rearrange("p (t m) -> p t m", t=4),
+                out_0[K_PASS * g:K_PASS * (g + 1), c * SWEEP:(c + 1) * SWEEP].rearrange("(p t) m -> p t m", t=PACK),
+                y[:].rearrange("p (t m) -> p t m", t=PACK),
             )
             return y
 
         def round_y(copy, y):
-            y_bf = ring.tile([P, 4 * HALF], BF16, name="y_bf", align_bytes=64, bufs=4)
-            copy(
-                y_bf[:].rearrange("p (m i t) -> p m t i", i=4, t=4),
-                y[:].rearrange("p (t m i) -> p m t i", t=4, i=4),
-            )
+            y_bf = ring.tile([P, PACK * SWEEP], BF16, name="y_bf", align_bytes=64, bufs=4)
+            copy(as_words(y_bf[:]), by_four(y[:]))
             return y_bf
 
-        def quantise_y(c, g, y_bf, y_codes):
+        y_planes = held([P, 2 * PAIRS], U8, "y_planes")
+        y_codes = [held([P, 2 * SWEEP], U32, "y_codes%d" % c) for c in range(2)]
+
+        def quantise_y(c, g, y_bf):
             nc.vector.quantize_mx(
-                y_codes[:, g * HALF:(g + 1) * HALF].bitcast(E4M3),
-                y_planes[:, g * PAIRS + c * HALF:g * PAIRS + (c + 1) * HALF], y_bf[:],
+                y_codes[c][:, g * SWEEP:(g + 1) * SWEEP].bitcast(E4M3),
+                y_planes[:, g * PAIRS + c * SWEEP:g * PAIRS + (c + 1) * SWEEP], y_bf[:],
             )
 
-        def store_codes(c, y_codes):
+        def store_codes(c):
             nc.sync.dma_start(
-                out_1.rearrange("g p m t -> p g (m t)").bitcast(I32)[:, :, c * HALF:(c + 1) * HALF],
-                y_codes[:].bitcast(I32).rearrange("p (g m) -> p g m", g=2),
+                out_1.rearrange("g p m t -> p g (m t)").bitcast(I32)[:, :, c * SWEEP:(c + 1) * SWEEP],
+                y_codes[c][:].bitcast(I32).rearrange("p (g m) -> p g m", g=2),
             )
 
-        y_codes = [held([P, 2 * HALF], U32, "y_codes%d" % c) for c in range(2)]
         z_bf0 = make_z(0)
         pick(0, 1)
         z0 = quantise_z(0, z_bf0)
-        y0 = [make_y(0, g, z0, False) for g in range(2)]
+        y0 = [make_y(0, g, z0, gain_on_scalar) for g in range(2)]
         y_bf0 = [round_y(nc.scalar.copy, y0[g]) for g in range(2)]
-        for t in range(1, 4):
+        for t in range(1, PACK):
             pick(t, 1)
         z1 = quantise_z(1, make_z(1))
         for g in range(2):
-            quantise_y(0, g, y_bf0[g], y_codes[0])
-        store_codes(0, y_codes[0])
-        y11 = make_y(1, 1, z1, True)
-        y10 = make_y(1, 0, z1, False)
+            quantise_y(0, g, y_bf0[g])
+        store_codes(0)
+        y11 = make_y(1, 1, z1, gain_on_vector)
+        y10 = make_y(1, 0, z1, gain_on_scalar)
         y_bf11 = round_y(nc.vector.tensor_copy, y11)
         y_bf10 = round_y(nc.scalar.copy, y10)
-        quantise_y(1, 1, y_bf11, y_codes[1])
-        quantise_y(1, 0, y_bf10, y_codes[1])
-        store_codes(1, y_codes[1])
-        for d in range(4):
-            queue = nc.sync if d % 2 == 0 else nc.scalar
-            queue.dma_start(
+        quantise_y(1, 1, y_bf11)
+        quantise_y(1, 0, y_bf10)
+        store_codes(1)
+        for d in range(QUADS):
+            (nc.sync, nc.scalar)[d % 2].dma_start(
                 out_2[:, 4 * d:4 * d + 4, :].bitcast(I32).rearrange("g r m -> r g m"),
                 y_planes[32 * d:32 * d + 4, :].bitcast(I32).rearrange("r (g m) -> r g m", g=2),
             )

from contextlib import ExitStack

import concourse.mybir as mybir

K, T, S, PAIRS, H, N = 1536, 2048, 1024, 512, 512, 1024
FLOPS = 2 * (2 * K * H * S + H * N * PAIRS)

F32 = mybir.dt.float32
BF16 = mybir.dt.bfloat16
I32 = mybir.dt.int32
U32 = mybir.dt.uint32
U16 = mybir.dt.uint16
U8 = mybir.dt.uint8
E4M3 = mybir.dt.float8_e4m3fn_x4
E2M1 = mybir.dt.float4_e2m1fn_x4
ACT = mybir.ActivationFunctionType
ALU = mybir.AluOpType

P = 128
PACK = 4
K_PASS = P * PACK
PASSES = K // K_PASS
BANK = 512
QUADS = 4
SWEEP = PAIRS // 2
LIST_ROWS = 16

PLANE_OF_PASS = (0, 2, 1)


def tile_list_still_cut_features_kernel(
    tc, tab_words, tab_scales, offs, w1_words, w1_scales, level, w2, pos1, pos2, allow, w3, rowgain,
    out_0, out_1, out_2,
):
    nc = tc.nc
    with ExitStack() as ctx:
        keep = ctx.enter_context(tc.tile_pool(name="keep", bufs=1))
        shared = ctx.enter_context(tc.tile_pool(name="shared", bufs=1))
        ring = ctx.enter_context(tc.tile_pool(name="ring", bufs=2))
        psum = ctx.enter_context(tc.psum_pool(name="psum", bufs=4))

        def held(shape, dtype, name):
            return keep.tile(shape, dtype, name=name, align_bytes=64)

        def after(tag, shape, dtype, name):
            return keep.tile(shape, dtype, name=name, tag=tag, align_bytes=64)

        def overlaid(offset, shape, dtype, name):
            return shared.tile(shape, dtype, name=name, align_bytes=64, offset=offset)

        offs_t = keep.tile([P, S // LIST_ROWS], U16, name="offs_t")
        pos1_t = keep.tile([P, PAIRS // LIST_ROWS], U16, name="pos1_t")
        pos2_t = keep.tile([P, PAIRS // LIST_ROWS], U16, name="pos2_t")
        nc.sync.dma_start(offs_t[:], offs)
        nc.sync.dma_start(pos1_t[:], pos1)
        nc.sync.dma_start(pos2_t[:], pos2)

        scale_window = overlaid(0, [P, T], U8, "scale_window")
        nc.gpsimd.memset(scale_window[:].bitcast(I32), 0)
        nc.scalar.dma_start(
            scale_window[0:P:4, :].bitcast(I32), tab_scales[0:2].bitcast(I32).rearrange("a q t -> q a t")
        )
        nc.scalar.dma_start(scale_window[2:P:8, :].bitcast(I32), tab_scales[2].bitcast(I32))

        warm_in = after("table_odd", [P, 1], F32, "warm_in")
        warm_bias = overlaid(T, [P, 1], F32, "warm_bias")
        warm_out = after("w2_first", [P, 1], F32, "warm_out")
        nc.gpsimd.memset(warm_in[:], 1.0)
        nc.gpsimd.memset(warm_bias[:], 0.0)
        nc.scalar.activation(warm_out[:], warm_in[:], ACT.Sqrt, bias=warm_bias[:])

        w1_planes_raw = held([P, PASSES * H], U8, "w1_planes_raw")
        nc.vector.memset(w1_planes_raw[:].bitcast(I32), 0)
        v_planes = held([P, 4 * S], U8, "v_planes")
        nc.vector.memset(v_planes[:, 0:PASSES * S].bitcast(I32), 0)
        for d in range(QUADS):
            nc.scalar.dma_start(
                w1_planes_raw[32 * d:32 * d + 4, :].bitcast(I32).rearrange("r (a c) -> r a c", a=PASSES),
                w1_scales[:, 4 * d:4 * d + 4, :].bitcast(I32).rearrange("a r c -> r a c"),
            )

        def load_table(a, words):
            nc.sync.dma_start(words[:], tab_words[a].rearrange("p t i -> p (t i)").bitcast(I32))
            return words

        def load_w2(a, raw):
            nc.sync.dma_start(raw[:], w2[K_PASS * a:K_PASS * (a + 1), :].rearrange("(p j) c -> p (j c)", j=PACK))
            return raw

        tab0 = load_table(0, after("table_even", [P, T], I32, "tab0"))
        w1_raw = held([P, PASSES * H // 2], I32, "w1_raw")
        nc.sync.dma_start(
            w1_raw[:].rearrange("p (a c) -> p a c", a=PASSES),
            w1_words.bitcast(I32).rearrange("a p c -> p a c"),
        )
        tab1 = load_table(1, after("table_odd", [P, T], I32, "tab1"))
        w2_raw0 = load_w2(0, after("w2_first", [P, PACK * H], F32, "w2_raw0"))

        scales_got = held([P, S], U8, "scales_got")
        nc.vector.tensor_copy(scales_got[:], scale_window[:].indirect(offs_t[:]))
        for d in range(QUADS):
            nc.scalar.dma_start(
                v_planes[32 * d:32 * d + 4, :].bitcast(I32), scales_got[32 * d:32 * d + 32:2, :].bitcast(I32)
            )

        v_words = [held([P, S], U32, "v_words%d" % a) for a in range(PASSES)]
        w1_codes = []
        w2_codes = [held([P, H], U32, "w2_codes%d" % a) for a in range(PASSES)]
        w2_planes = [held([P, H], U8, "w2_planes%d" % a) for a in range(PASSES)]

        def gather_words(a, words, lo, hi):
            nc.vector.tensor_copy(
                v_words[a][:, lo:hi], words[:].bitcast(U32).indirect(offs_t[:, lo // LIST_ROWS:hi // LIST_ROWS])
            )

        def deal_w1(pair, codes):
            nc.vector.tensor_copy(
                codes[:].rearrange("p (a t q w) -> p a t q w", a=PASSES, t=2, w=4),
                w1_raw[:].rearrange("p (a q t w) -> p a t q w", a=PASSES, t=PACK, w=4)[:, :, 2 * pair:2 * pair + 2],
            )
            w1_codes.append(codes)

        def round_pass_on_scalar(raw, w2_bf):
            nc.scalar.copy(
                w2_bf[:].rearrange("p (t q i j) -> p t q j i", q=16, i=8, j=PACK),
                raw[:].rearrange("p (j q t i) -> p t q j i", j=PACK, t=PACK, i=8),
            )
            return w2_bf

        def round_tile_on_vector(raw, t, w2_bf):
            nc.vector.tensor_copy(
                w2_bf.rearrange("p (q e i j) -> p q e j i", e=2, i=4, j=PACK),
                raw[:].rearrange("p (j q t e i) -> p t q e j i", j=PACK, t=PACK, e=2, i=4)[:, t],
            )

        def quantise_w2(a, lo, hi, w2_bf):
            nc.vector.quantize_mx(
                w2_codes[a][:, lo * P:hi * P].bitcast(E4M3), w2_planes[a][:, lo * P:hi * P], w2_bf[:]
            )

        tab2 = load_table(2, overlaid(0, [P, T], I32, "tab2"))
        gather_words(0, tab0, 0, S)
        w2_raw1 = load_w2(1, after("table_even", [P, PACK * H], F32, "w2_raw1"))
        deal_w1(0, held([P, PASSES * H // 4], I32, "w1_codes0"))
        w1_planes = held([P, PASSES * H], U8, "w1_planes")
        nc.vector.tensor_copy(
            w1_planes[:].bitcast(I32).rearrange("p (a t q w) -> p a t q w", a=PASSES, t=PACK, w=2),
            w1_planes_raw[:].bitcast(I32).rearrange("p (a q t w) -> p a t q w", a=PASSES, t=PACK, w=2),
        )

        row_constants = held([P, 40], F32, "row_constants")
        with nc.allow_non_contiguous_dma(reason="one value a partition"):
            for t in range(PACK):
                nc.gpsimd.dma_start(
                    row_constants[:, 8 * t:8 * t + 1], level.rearrange("(q t i) -> t q i", t=PACK, i=8)[t]
                )
        gains = row_constants[:, 32:40]
        nc.gpsimd.dma_start(
            gains.rearrange("p (g t) -> p g t", g=2), rowgain.rearrange("(g p t) -> p g t", g=2, t=PACK)
        )

        gather_words(1, tab1, 0, S)

        w2_bf0 = round_pass_on_scalar(w2_raw0, held([P, PACK * H], BF16, "w2_bf0"))
        w2_raw2 = load_w2(2, after("table_odd", [P, PACK * H], F32, "w2_raw2"))
        allow_t = after("w2_first", [P, PACK * PAIRS], F32, "allow_t")
        for t in range(PACK):
            nc.sync.dma_start(
                allow_t[:, t * PAIRS:(t + 1) * PAIRS], allow.rearrange("(q t i) m -> t q (i m)", t=PACK, i=8)[t]
            )
        gather_words(2, tab2, 0, BANK)
        gather_words(2, tab2, BANK, S)
        w2_bf1 = held([P, PACK * H], BF16, "w2_bf1")
        for t in range(PACK):
            round_tile_on_vector(w2_raw1, t, w2_bf1[:, t * K_PASS:(t + 1) * K_PASS])
        quantise_w2(0, 0, PACK, w2_bf0)
        quantise_w2(1, 0, PACK, w2_bf1)
        last_bf0 = held([P, K_PASS], BF16, "last_bf0")
        last_bf1 = after("w2_last", [P, K_PASS], BF16, "last_bf1")
        last_bf23 = held([P, 2 * K_PASS], BF16, "last_bf23")
        round_tile_on_vector(w2_raw2, 0, last_bf0[:])
        round_tile_on_vector(w2_raw2, 1, last_bf1[:])
        quantise_w2(2, 0, 1, last_bf0)
        quantise_w2(2, 1, 2, last_bf1)
        deal_w1(1, after("w2_last", [P, PASSES * H // 4], I32, "w1_codes1"))
        round_tile_on_vector(w2_raw2, 2, last_bf23[:, 0:K_PASS])
        round_tile_on_vector(w2_raw2, 3, last_bf23[:, K_PASS:2 * K_PASS])
        quantise_w2(2, 2, PACK, last_bf23)
        w3_raw = after("table_even", [P, PACK * N], F32, "w3_raw")
        for t in range(PACK):
            nc.sync.dma_start(w3_raw[:, t * N:(t + 1) * N], w3.rearrange("(q t i) n -> t q (i n)", t=PACK, i=8)[t])

        def product(tag, half, weight):
            acc = psum.tile([P, BANK], F32, name=tag, tag=tag)
            for a in range(PASSES):
                codes, plane = weight(a)
                plane_lo = PLANE_OF_PASS[a] * S + half * BANK
                nc.tensor.matmul_mx(
                    acc[:], lhsT=codes, lhsT_scale=plane,
                    rhs=v_words[a][:, half * BANK:(half + 1) * BANK].bitcast(E4M3),
                    rhs_scale=v_planes[:, plane_lo:plane_lo + BANK],
                    start=(a == 0), stop=(a == PASSES - 1),
                )
            return acc

        root = [held([P, S], F32, "root%d" % t) for t in range(PACK)]
        h = [held([P, S], F32, "h%d" % t) for t in range(PACK)]
        cut1 = [held([P, PACK * SWEEP], F32, "cut1_0")]
        cut2 = [held([P, PACK * SWEEP], F32, "cut2_0")]

        def make_root(t, width):
            def w1_operand(a):
                lo = 2 * (2 * a + t % 2) * P
                codes = w1_codes[t // 2][:].bitcast(U8)[:, lo:lo + 2 * P].bitcast(E2M1)
                return codes, w1_planes[:, a * H + t * P:a * H + (t + 1) * P]

            size = ring.tile([P, S], F32, name="size")
            for half in range(2):
                hi = (half + 1) * BANK
                nc.scalar.activation(size[:, hi - BANK:hi], product("w1_sum", half, w1_operand)[:], ACT.Abs)
                if hi % width == 0:
                    nc.scalar.activation(
                        root[t][:, hi - width:hi], size[:, hi - width:hi], ACT.Sqrt,
                        bias=row_constants[:, 8 * t:8 * t + 1],
                    )

        def make_h(t):
            def w2_operand(a):
                return w2_codes[a][:, t * P:(t + 1) * P].bitcast(E4M3), w2_planes[a][:, t * P:(t + 1) * P]

            for half in range(2):
                cols = slice(half * BANK, (half + 1) * BANK)
                nc.vector.tensor_tensor(h[t][:, cols], product("w2_sum", half, w2_operand)[:], root[t][:, cols], ALU.add)

        def pick(t, c):
            lo, hi = c * SWEEP, (c + 1) * SWEEP
            place = slice(t * SWEEP, (t + 1) * SWEEP)
            nc.vector.tensor_tensor(
                cut1[c][:, place], h[t][:].indirect(pos1_t[:, lo // LIST_ROWS:hi // LIST_ROWS]),
                allow_t[:, t * PAIRS + lo:t * PAIRS + hi], ALU.add,
            )
            nc.vector.tensor_copy(cut2[c][:, place], h[t][:].indirect(pos2_t[:, lo // LIST_ROWS:hi // LIST_ROWS]))

        make_root(0, BANK)
        make_root(1, S)
        for t in range(PACK):
            if 0 < t < PACK - 1:
                make_root(t + 1, S)
            make_h(t)
            pick(t, 0)

        w3_codes = held([P, N], U32, "w3_codes")
        w3_planes = held([P, N], U8, "w3_planes")
        for g in range(2):
            w3_bf = after("w3_bf%d" % g, [P, PACK * K_PASS], BF16, "w3_bf%d" % g)
            nc.scalar.copy(
                w3_bf[:].rearrange("p (t m j) -> p m j t", t=PACK, j=PACK),
                w3_raw[:].rearrange("p (j g m t) -> p g m j t", j=PACK, g=2, t=PACK)[:, g],
            )
            cols = slice(g * K_PASS, (g + 1) * K_PASS)
            nc.vector.quantize_mx(w3_codes[:, cols].bitcast(E4M3), w3_planes[:, cols], w3_bf[:])

        cut1.append(after("w3_bf0", [P, PACK * SWEEP], F32, "cut1_1"))
        cut2.append(after("w3_bf1", [P, PACK * SWEEP], F32, "cut2_1"))

        def by_four(ap):
            return ap.rearrange("p (t m i) -> p m t i", t=PACK, i=4)

        def as_words(ap):
            return ap.rearrange("p (m i t) -> p m t i", i=4, t=PACK)

        def make_z(c):
            z_bf = ring.tile([P, PACK * SWEEP], BF16, name="z_bf", align_bytes=64)
            nc.vector.tensor_tensor(as_words(z_bf[:]), by_four(cut1[c][:]), by_four(cut2[c][:]), ALU.min)
            return z_bf

        def quantise_z(c, z_bf):
            z_codes = held([P, SWEEP], U32, "z_codes%d" % c)
            z_plane = held([P, SWEEP], U8, "z_plane%d" % c)
            nc.vector.quantize_mx(z_codes[:].bitcast(E4M3), z_plane[:], z_bf[:])
            return z_codes, z_plane

        def gain_on_scalar(out, acc, gain):
            nc.scalar.activation(out, acc, ACT.Copy, scale=gain)

        def gain_on_vector(out, acc, gain):
            nc.vector.tensor_scalar(out, acc, gain, None, ALU.mult)

        def make_y(c, g, z, apply_gain):
            z_codes, z_plane = z
            y = held([P, PACK * SWEEP], F32, "y%d%d" % (c, g))
            for bank in range(2):
                acc = psum.tile([P, BANK], F32, name="y_sum", tag=("w1_sum", "w2_sum")[g])
                for side in range(2):
                    u = PACK * g + 2 * bank + side
                    nc.tensor.matmul_mx(
                        acc[:, side * SWEEP:(side + 1) * SWEEP],
                        lhsT=w3_codes[:, u * P:(u + 1) * P].bitcast(E4M3), lhsT_scale=w3_planes[:, u * P:(u + 1) * P],
                        rhs=z_codes[:].bitcast(E4M3), rhs_scale=z_plane[:], start=True, stop=True,
                    )
                for side in range(2):
                    t = 2 * bank + side
                    apply_gain(
                        y[:, t * SWEEP:(t + 1) * SWEEP], acc[:, side * SWEEP:(side + 1) * SWEEP],
                        gains[:, PACK * g + t:PACK * g + t + 1],
                    )
            nc.sync.dma_start(
                out_0[K_PASS * g:K_PASS * (g + 1), c * SWEEP:(c + 1) * SWEEP].rearrange("(p t) m -> p t m", t=PACK),
                y[:].rearrange("p (t m) -> p t m", t=PACK),
            )
            return y

        def round_y(copy, y):
            y_bf = ring.tile([P, PACK * SWEEP], BF16, name="y_bf", align_bytes=64, bufs=4)
            copy(as_words(y_bf[:]), by_four(y[:]))
            return y_bf

        y_planes = held([P, 2 * PAIRS], U8, "y_planes")
        y_codes = [held([P, 2 * SWEEP], U32, "y_codes%d" % c) for c in range(2)]

        def quantise_y(c, g, y_bf):
            nc.vector.quantize_mx(
                y_codes[c][:, g * SWEEP:(g + 1) * SWEEP].bitcast(E4M3),
                y_planes[:, g * PAIRS + c * SWEEP:g * PAIRS + (c + 1) * SWEEP], y_bf[:],
            )

        def store_codes(c):
            nc.sync.dma_start(
                out_1.rearrange("g p m t -> p g (m t)").bitcast(I32)[:, :, c * SWEEP:(c + 1) * SWEEP],
                y_codes[c][:].bitcast(I32).rearrange("p (g m) -> p g m", g=2),
            )

        z_bf0 = make_z(0)
        pick(0, 1)
        z0 = quantise_z(0, z_bf0)
        y0 = [make_y(0, g, z0, gain_on_scalar) for g in range(2)]
        y_bf0 = [round_y(nc.scalar.copy, y0[g]) for g in range(2)]
        for t in range(1, PACK):
            pick(t, 1)
        z1 = quantise_z(1, make_z(1))
        for g in range(2):
            quantise_y(0, g, y_bf0[g])
        store_codes(0)
        y11 = make_y(1, 1, z1, gain_on_vector)
        y10 = make_y(1, 0, z1, gain_on_scalar)
        y_bf11 = round_y(nc.vector.tensor_copy, y11)
        y_bf10 = round_y(nc.scalar.copy, y10)
        quantise_y(1, 1, y_bf11)
        quantise_y(1, 0, y_bf10)
        store_codes(1)
        for d in range(QUADS):
            (nc.sync, nc.scalar)[d % 2].dma_start(
                out_2[:, 4 * d:4 * d + 4, :].bitcast(I32).rearrange("g r m -> r g m"),
                y_planes[32 * d:32 * d + 4, :].bitcast(I32).rearrange("r (g m) -> r g m", g=2),
            )
